import numpy as np
import ml_dtypes


def mxq(x, axis, fmt="e4m3"):
    dtype, down = {"e4m3": (ml_dtypes.float8_e4m3fn, 7), "e5m2": (ml_dtypes.float8_e5m2, 14)}[fmt]
    v = np.moveaxis(np.asarray(x, np.float32).astype(ml_dtypes.bfloat16).astype(np.float64), axis, -1)
    blocks = v.reshape(v.shape[:-1] + (-1, 32))
    amax = np.abs(blocks).max(-1, keepdims=True)
    byte = np.maximum(np.where(amax > 0, np.frexp(amax)[1] - 1 + 127, 0) - down, 1)
    scale = np.exp2(byte - 127.0)
    codes = (blocks / scale).astype(np.float32).astype(dtype).astype(np.float64)
    return np.moveaxis((codes * scale).reshape(v.shape), -1, axis)


WIDE = False


def mx_kscale(k):
    if not WIDE:
        return np.ones(k)
    levels = np.array([10, -10, 5, -5, 0])
    if k % 512:
        return np.exp2(np.random.permutation(np.resize(levels, k // 32))).repeat(32)
    a = np.empty((k // 512, 16))
    for p in range(k // 512):
        a[p, :8] = np.random.permutation(np.resize(levels, 8))
        for g in range(8):
            far = levels[np.abs(levels - a[p, g]) >= 10]
            a[p, g + 8] = far[np.random.randint(len(far))]
    return np.exp2(a.ravel()).repeat(32)


def f64(x):
    return np.asarray(x).astype(np.float64)


def striped(idx):
    return np.tile(idx.reshape(-1, 16).T, (8, 1)).astype(np.uint16)


def unstriped(offs):
    return offs[:16].T.reshape(-1).astype(np.int64)


def pack_weight(w):
    k, n = w.shape
    w = f64(np.asarray(w, np.float32).astype(ml_dtypes.bfloat16)).reshape(k // 32, 32, n)
    amax = np.abs(w).max(1)
    byte = np.clip(np.where(amax > 0, np.frexp(amax)[1] - 1 + 127 - 7, 1), 1, 254)
    scaled = (w * np.exp2(127.0 - byte)[:, None, :]).reshape(k, n).astype(np.float32)
    words = np.ascontiguousarray(scaled.reshape(k // 512, 128, 4, n).transpose(0, 1, 3, 2)).astype(ml_dtypes.float8_e4m3fn).view(np.uint8)
    return words, np.ascontiguousarray(byte.astype(np.uint8).reshape(k // 512, 16, n))


def unpack_weight(words, scales):
    g, p, n, _ = words.shape
    vals = np.ascontiguousarray(words).view(ml_dtypes.float8_e4m3fn).astype(np.float64) * np.repeat(np.exp2(scales.astype(np.float64) - 127.0), 8, axis=1)[..., None]
    return vals.transpose(0, 1, 3, 2).reshape(g * 512, n)


def relu(v):
    return np.maximum(v, 0.0)


def sigmoid(v):
    return 1.0 / (1.0 + np.exp(-np.maximum(v, -700.0)))


K, T, S, V, H, W = 512, 2048, 512, 512, 512, 1024


def setup_inputs():
    n = np.random.standard_normal
    s = mx_kscale(K)[:, None]
    u = mx_kscale(H)
    packed_xT = pack_weight(n((K, T)) * s)
    packed_eT = pack_weight(n((K, W)) / np.sqrt(2 * K) / s)
    return {
        "x_words": packed_xT[0],
        "x_scales": packed_xT[1],
        "e_words": packed_eT[0],
        "e_scales": packed_eT[1],
        "w1": (n((K, H)) / np.sqrt(K) / s * u).astype(np.float32),
        "w2": (n((K, H)) / np.sqrt(K) * np.sqrt(2 * K) * s / u / np.sqrt(2 * H)).astype(np.float32),
        "offs": striped(np.random.permutation(T)[:S]),
        "cand": striped(np.random.permutation(W)[:V]),
    }


def reference(x_words, x_scales, e_words, e_scales, w1, w2, offs, cand):
    xq = unpack_weight(x_words, x_scales)[:, unstriped(offs)]
    p = relu(mxq(f64(w1), 0, "e4m3").T @ xq)
    e_cand = unpack_weight(e_words, e_scales)[:, unstriped(cand)]
    d = relu(mxq(f64(w2), 0, "e4m3").T @ e_cand)
    y = mxq(p, 0, "e4m3").T @ mxq(d, 0, "e4m3") + xq.T @ e_cand
    return sigmoid(y)

@@ -1,0 +1,148 @@
+from contextlib import ExitStack
+
+import concourse.mybir as mybir
+
+K, T, S, V, H, W = 512, 2048, 512, 512, 512, 1024
+FLOPS = 4 * 2 * 512 * 512 * 512
+
+F32 = mybir.dt.float32
+BF16 = mybir.dt.bfloat16
+I32 = mybir.dt.int32
+U32 = mybir.dt.uint32
+U16 = mybir.dt.uint16
+U8 = mybir.dt.uint8
+FP8X4 = mybir.dt.float8_e4m3fn_x4
+ACT = mybir.ActivationFunctionType
+
+P = 128
+PACK = 4
+BLOCKS = 4
+HALF = H // 2
+
+
+def tile_picked_zneumf_sig_p_kernel(
+    tc, x_words, x_scales, e_words, e_scales, w1, w2, offs, cand, out
+):
+    nc = tc.nc
+    with ExitStack() as ctx:
+        keep = ctx.enter_context(tc.tile_pool(name="keep", bufs=1))
+        psum = ctx.enter_context(tc.psum_pool(name="psum", bufs=1))
+
+        def sbuf(name, shape, dtype):
+            return keep.tile(shape, dtype, name=name, align_bytes=64)
+
+        cand_list = keep.tile([P, V // 16], U16, name="cand_list")
+        offs_list = keep.tile([P, S // 16], U16, name="offs_list")
+        e_scale_table = sbuf("e_scale_table", [P, W], U8)
+        x_scale_table = sbuf("x_scale_table", [P, T], U8)
+        e_word_table = sbuf("e_word_table", [P, W], U32)
+        x_word_table = sbuf("x_word_table", [P, T], U32)
+        warm = sbuf("warm", [P, 2], F32)
+
+        nc.vector.memset(e_scale_table[:].bitcast(I32), 0)
+        nc.vector.memset(x_scale_table[:].bitcast(I32), 0)
+        nc.vector.memset(warm[:, 0:1], 0.0)
+        nc.scalar.activation(warm[:, 1:2], warm[:, 0:1], ACT.Sigmoid)
+
+        def load_scales(queue, table, scales):
+            for q in range(4):
+                queue.dma_start(
+                    out=table[32 * q : 32 * q + 4, :].bitcast(I32),
+                    in_=scales[0, 4 * q : 4 * q + 4, :].bitcast(I32),
+                )
+
+        def load_words(table, words):
+            nc.sync.dma_start(out=table[:].bitcast(I32), in_=words[0].rearrange("p n t -> p (n t)").bitcast(I32))
+
+        def load_weight(name, w, a, b):
+            raw = sbuf(name, [P, PACK, b - a], F32)
+            nc.sync.dma_start(out=raw[:], in_=w.rearrange("(p j) c -> p j c", j=PACK)[:, :, a:b])
+            return raw
+
+        def round_weight(copy, grouped, raw, first, a, b):
+            words = grouped[:, :, a // PACK : b // PACK, :]
+            copy(
+                words.rearrange("p s (u r) j -> p s u j r", r=4),
+                raw[:, :, a - first : b - first].rearrange("p j (u s r) -> p s u j r", s=PACK, r=4),
+            )
+
+        def quantize(codes, scales, values):
+            nc.vector.quantize_mx(out=codes.bitcast(FP8X4), scales=scales, in_=values)
+
+        def mx(acc, lhs, lhs_scale, rhs, rhs_scale, start, stop):
+            nc.tensor.matmul_mx(
+                out=acc, lhsT=lhs.bitcast(FP8X4), lhsT_scale=lhs_scale, rhs=rhs.bitcast(FP8X4), rhs_scale=rhs_scale,
+                start=start, stop=stop,
+            )
+
+        def gather(dst, table, offsets, a, b):
+            nc.vector.tensor_copy(dst[:, a:b], table[:].indirect(offsets[:, a // 16 : b // 16]))
+
+        def relu_scalar(dst, src):
+            nc.scalar.activation(dst, src, ACT.Relu)
+
+        def relu_vector(dst, src):
+            nc.vector.tensor_scalar_max(dst, src, 0.0)
+
+        def tower_block(name, tag, w_codes, w_scales, codes, scales, b, relu):
+            cols = slice(b * P, (b + 1) * P)
+            acc = psum.tile([P, PACK, P], F32, name=name + "_acc", tag=tag)
+            for s in range(PACK):
+                slot = slice(s * P, (s + 1) * P)
+                mx(acc[:, s, :], w_codes[:, slot], w_scales[:, slot], codes[:, cols], scales[:, cols], True, True)
+            hidden = sbuf(name + "_hidden", [P, P, PACK], BF16)
+            relu(hidden[:], acc[:].rearrange("p s t -> p t s"))
+            return hidden
+
+        e_codes = sbuf("e_codes", [P, V], U32)
+        e_plane = sbuf("e_plane", [P, V], U8)
+        x_codes = sbuf("x_codes", [P, S], U32)
+        x_plane = sbuf("x_plane", [P, S], U8)
+        w1_grouped = sbuf("w1_grouped", [P, PACK, P, PACK], BF16)
+        w2_grouped = sbuf("w2_grouped", [P, PACK, P, PACK], BF16)
+        w1_codes = sbuf("w1_codes", [P, H], U32)
+        w1_plane = sbuf("w1_plane", [P, H], U8)
+        w2_codes = sbuf("w2_codes", [P, H], U32)
+        w2_plane = sbuf("w2_plane", [P, H], U8)
+        d_codes = sbuf("d_codes", [P, V], U32)
+        p_codes = sbuf("p_codes", [P, S], U32)
+        p_plane = sbuf("p_plane", [P, S], U8)
+
+        nc.sync.dma_start(cand_list[:], cand)
+        nc.sync.dma_start(offs_list[:], offs)
+        load_words(e_word_table, e_words)
+        load_scales(nc.sync, e_scale_table, e_scales)
+        w2_raw = load_weight("w2_raw", w2, 0, H)
+        load_scales(nc.sync, x_scale_table, x_scales)
+        w1_raw = load_weight("w1_raw", w1, 0, H)
+        load_words(x_word_table, x_words)
+
+        gather(e_plane, e_scale_table, cand_list, 0, V)
+        gather(e_codes, e_word_table, cand_list, 0, V)
+        round_weight(nc.scalar.copy, w2_grouped, w2_raw, 0, 0, 192)
+        round_weight(nc.vector.tensor_copy, w2_grouped, w2_raw, 0, 192, H)
+        quantize(w2_codes[:], w2_plane[:], w2_grouped[:].rearrange("p s m j -> p (s m j)"))
+        gather(x_plane, x_scale_table, offs_list, 0, S)
+        round_weight(nc.vector.tensor_copy, w1_grouped, w1_raw, 0, 0, H)
+        d_hidden = [
+            tower_block("d%d" % b, "low%d" % b, w2_codes, w2_plane, e_codes, e_plane, b, relu_scalar) for b in range(BLOCKS)
+        ]
+        quantize(w1_codes[:], w1_plane[:], w1_grouped[:].rearrange("p s m j -> p (s m j)"))
+        for b in range(BLOCKS):
+            cols = slice(b * P, (b + 1) * P)
+            quantize(d_codes[:, cols], w1_plane[4:P, cols], d_hidden[b][:].rearrange("p t s -> p (t s)"))
+        gather(x_codes, x_word_table, offs_list, 0, S // 2)
+        gather(x_codes, x_word_table, offs_list, S // 2, S)
+        p_hidden = [
+            tower_block("p%d" % b, "high%d" % b, w1_codes, w1_plane, x_codes, x_plane, b, relu_vector if b % 2 else relu_scalar)
+            for b in range(BLOCKS)
+        ]
+        for b in range(BLOCKS):
+            cols = slice(b * P, (b + 1) * P)
+            y = psum.tile([P, V], F32, name="y%d" % b, tag="low%d" % b)
+            mx(y[:], x_codes[:, cols], x_plane[:, cols], e_codes[:], e_plane[:], True, False)
+            quantize(p_codes[:, cols], p_plane[:, cols], p_hidden[b][:].rearrange("p t s -> p (t s)"))
+            mx(y[:], p_codes[:, cols], p_plane[:, cols], d_codes[:], w1_plane[4:P, :], False, True)
+            scores = sbuf("scores%d" % b, [P, V], F32)
+            nc.scalar.activation(scores[:], y[:], ACT.Sigmoid)
+            nc.sync.dma_start(out=out[cols, :], in_=scores[:])

@@ -44,11 +44,11 @@ def tile_picked_zneumf_sig_p_kernel(
         nc.vector.memset(warm[:, 0:1], 0.0)
         nc.scalar.activation(warm[:, 1:2], warm[:, 0:1], ACT.Sigmoid)
 
-        def load_scales(queue, table, scales):
-            for q in range(4):
-                queue.dma_start(
-                    out=table[32 * q : 32 * q + 4, :].bitcast(I32),
-                    in_=scales[0, 4 * q : 4 * q + 4, :].bitcast(I32),
+        def load_scales(table, first, scales):
+            for r in range(4):
+                nc.sync.dma_start(
+                    out=table[first + r : P : 32, :].bitcast(I32),
+                    in_=scales[0].rearrange("(q r) c -> r q c", r=4)[r].bitcast(I32),
                 )
 
         def load_words(table, words):
@@ -59,11 +59,11 @@ def tile_picked_zneumf_sig_p_kernel(
             nc.sync.dma_start(out=raw[:], in_=w.rearrange("(p j) c -> p j c", j=PACK)[:, :, a:b])
             return raw
 
-        def round_weight(copy, grouped, raw, first, a, b):
-            words = grouped[:, :, a // PACK : b // PACK, :]
+        def round_weight(copy, grouped, raw, first, a, b, slots=slice(0, PACK)):
+            words = grouped[:, slots, a // PACK : b // PACK, :]
             copy(
                 words.rearrange("p s (u r) j -> p s u j r", r=4),
-                raw[:, :, a - first : b - first].rearrange("p j (u s r) -> p s u j r", s=PACK, r=4),
+                raw[:, :, a - first : b - first].rearrange("p j (u s r) -> p s u j r", s=PACK, r=4)[:, slots],
             )
 
         def quantize(codes, scales, values):
@@ -76,7 +76,7 @@ def tile_picked_zneumf_sig_p_kernel(
             )
 
         def gather(dst, table, offsets, a, b):
-            nc.vector.tensor_copy(dst[:, a:b], table[:].indirect(offsets[:, a // 16 : b // 16]))
+            nc.vector.tensor_copy(dst, table[:].indirect(offsets[:, a // 16 : b // 16]))
 
         def relu_scalar(dst, src):
             nc.scalar.activation(dst, src, ACT.Relu)
@@ -84,65 +84,76 @@ def tile_picked_zneumf_sig_p_kernel(
         def relu_vector(dst, src):
             nc.vector.tensor_scalar_max(dst, src, 0.0)
 
-        def tower_block(name, tag, w_codes, w_scales, codes, scales, b, relu):
-            cols = slice(b * P, (b + 1) * P)
-            acc = psum.tile([P, PACK, P], F32, name=name + "_acc", tag=tag)
+        def tower_block(name, tag, w_codes, w_scales, codes, scales):
+            acc = psum.tile([P, PACK, P], F32, name=name, tag=tag)
             for s in range(PACK):
                 slot = slice(s * P, (s + 1) * P)
-                mx(acc[:, s, :], w_codes[:, slot], w_scales[:, slot], codes[:, cols], scales[:, cols], True, True)
-            hidden = sbuf(name + "_hidden", [P, P, PACK], BF16)
-            relu(hidden[:], acc[:].rearrange("p s t -> p t s"))
-            return hidden
+                mx(acc[:, s, :], w_codes[:, slot], w_scales[:, slot], codes, scales, True, True)
+            return acc[:].rearrange("p s t -> p t s")
 
         e_codes = sbuf("e_codes", [P, V], U32)
-        e_plane = sbuf("e_plane", [P, V], U8)
+        e_tile = sbuf("e_tile", [P, V], U8)
         x_codes = sbuf("x_codes", [P, S], U32)
-        x_plane = sbuf("x_plane", [P, S], U8)
         w1_grouped = sbuf("w1_grouped", [P, PACK, P, PACK], BF16)
         w2_grouped = sbuf("w2_grouped", [P, PACK, P, PACK], BF16)
         w1_codes = sbuf("w1_codes", [P, H], U32)
         w1_plane = sbuf("w1_plane", [P, H], U8)
         w2_codes = sbuf("w2_codes", [P, H], U32)
         w2_plane = sbuf("w2_plane", [P, H], U8)
-        d_codes = sbuf("d_codes", [P, V], U32)
+        d_plane = sbuf("d_plane", [P, V], U8)
         p_codes = sbuf("p_codes", [P, S], U32)
         p_plane = sbuf("p_plane", [P, S], U8)
 
+        load_words(e_word_table, e_words)
         nc.sync.dma_start(cand_list[:], cand)
         nc.sync.dma_start(offs_list[:], offs)
-        load_words(e_word_table, e_words)
-        load_scales(nc.sync, e_scale_table, e_scales)
+        load_scales(e_scale_table, 4, e_scales)
         w2_raw = load_weight("w2_raw", w2, 0, H)
-        load_scales(nc.sync, x_scale_table, x_scales)
+        load_scales(x_scale_table, 0, x_scales)
         w1_raw = load_weight("w1_raw", w1, 0, H)
         load_words(x_word_table, x_words)
 
-        gather(e_plane, e_scale_table, cand_list, 0, V)
-        gather(e_codes, e_word_table, cand_list, 0, V)
-        round_weight(nc.scalar.copy, w2_grouped, w2_raw, 0, 0, 192)
-        round_weight(nc.vector.tensor_copy, w2_grouped, w2_raw, 0, 192, H)
+        gather(e_codes[:], e_word_table, cand_list, 0, V)
+        gather(e_tile[:], e_scale_table, cand_list, 0, V)
+        e_plane = e_tile[4:P, :]
+        round_weight(nc.scalar.copy, w2_grouped, w2_raw, 0, 0, 256)
+        round_weight(nc.vector.tensor_copy, w2_grouped, w2_raw, 0, 256, H)
+        x_plane_a = sbuf("x_plane_a", [P, S // 2], U8)
+        gather(x_plane_a[:], x_scale_table, offs_list, 0, S // 2)
         quantize(w2_codes[:], w2_plane[:], w2_grouped[:].rearrange("p s m j -> p (s m j)"))
-        gather(x_plane, x_scale_table, offs_list, 0, S)
-        round_weight(nc.vector.tensor_copy, w1_grouped, w1_raw, 0, 0, H)
-        d_hidden = [
-            tower_block("d%d" % b, "low%d" % b, w2_codes, w2_plane, e_codes, e_plane, b, relu_scalar) for b in range(BLOCKS)
+        x_plane_b = keep.tile([P, S // 2], U8, name="x_plane_b", tag="w2_grouped", align_bytes=64)
+        gather(x_plane_b[:], x_scale_table, offs_list, S // 2, S)
+        x_planes = [x_plane_a[:, 0:P], x_plane_a[:, P : 2 * P], x_plane_b[:, 0:P], x_plane_b[:, P : 2 * P]]
+        for h in range(2):
+            round_weight(nc.vector.tensor_copy, w1_grouped, w1_raw, 0, 0, H, slice(2 * h, 2 * h + 2))
+        for h in range(2):
+            cols = slice(h * HALF, (h + 1) * HALF)
+            quantize(w1_codes[:, cols], w1_plane[:, cols], w1_grouped[:, 2 * h : 2 * h + 2].rearrange("p s m j -> p (s m j)"))
+        d_hidden = sbuf("d_hidden", [P, V, PACK], BF16)
+        blocks = [slice(b * P, (b + 1) * P) for b in range(BLOCKS)]
+        for b, cols in enumerate(blocks):
+            acc = tower_block("d_acc%d" % b, "low%d" % b, w2_codes, w2_plane, e_codes[:, cols], e_plane[:, cols])
+            relu_scalar(d_hidden[:, cols, :], acc)
+
+        gather(x_codes[:, 0 : S // 2], x_word_table, offs_list, 0, S // 2)
+        gather(x_codes[:, S // 2 : S], x_word_table, offs_list, S // 2, S)
+        d_codes = keep.tile([P, V], U32, name="d_codes", tag="x_word_table", align_bytes=64)
+        quantize(d_codes[:], d_plane[:], d_hidden[:].rearrange("p t s -> p (t s)"))
+        p_hidden = [sbuf("p_hidden%d" % b, [P, P, PACK], BF16) for b in range(BLOCKS)]
+        p_acc = [
+            tower_block("p_acc%d" % b, "high%d" % b, w1_codes, w1_plane, x_codes[:, cols], x_planes[b])
+            for b, cols in enumerate(blocks)
         ]
-        quantize(w1_codes[:], w1_plane[:], w1_grouped[:].rearrange("p s m j -> p (s m j)"))
-        for b in range(BLOCKS):
-            cols = slice(b * P, (b + 1) * P)
-            quantize(d_codes[:, cols], w1_plane[4:P, cols], d_hidden[b][:].rearrange("p t s -> p (t s)"))
-        gather(x_codes, x_word_table, offs_list, 0, S // 2)
-        gather(x_codes, x_word_table, offs_list, S // 2, S)
-        p_hidden = [
-            tower_block("p%d" % b, "high%d" % b, w1_codes, w1_plane, x_codes, x_plane, b, relu_vector if b % 2 else relu_scalar)
-            for b in range(BLOCKS)
-        ]
-        for b in range(BLOCKS):
-            cols = slice(b * P, (b + 1) * P)
-            y = psum.tile([P, V], F32, name="y%d" % b, tag="low%d" % b)
-            mx(y[:], x_codes[:, cols], x_plane[:, cols], e_codes[:], e_plane[:], True, False)
+        for b in range(BLOCKS - 1):
+            relu_scalar(p_hidden[b][:], p_acc[b])
+        for b, cols in enumerate(blocks):
+            y = psum.tile([P, V], F32, name="y%d" % b, tag="high%d" % b if b else "low0")
+            mx(y[:], x_codes[:, cols], x_planes[b], e_codes[:], e_plane, True, False)
             quantize(p_codes[:, cols], p_plane[:, cols], p_hidden[b][:].rearrange("p t s -> p (t s)"))
-            mx(y[:], p_codes[:, cols], p_plane[:, cols], d_codes[:], w1_plane[4:P, :], False, True)
+            if b < 2:
+                half = slice(b * P // 2, (b + 1) * P // 2)
+                relu_vector(p_hidden[BLOCKS - 1][:, half, :], p_acc[BLOCKS - 1][:, half, :])
+            mx(y[:], p_codes[:, cols], p_plane[:, cols], d_codes[:], d_plane[:], False, True)
             scores = sbuf("scores%d" % b, [P, V], F32)
             nc.scalar.activation(scores[:], y[:], ACT.Sigmoid)
             nc.sync.dma_start(out=out[cols, :], in_=scores[:])

@@ -134,7 +134,9 @@ def tile_picked_zneumf_sig_p_kernel(
         for b, cols in enumerate(blocks):
             acc = tower_block("d_acc%d" % b, "low%d" % b, w2_codes, w2_plane, e_codes[:, cols], e_plane[:, cols])
             relu_scalar(d_hidden[:, cols, :], acc)
-
+        warm_acc = psum.tile([P, H], F32, name="warm_acc", tag="high3")
+        for w in range(2):
+            mx(warm_acc[:], w1_codes[:, 0:P], w1_plane[:, 0:P], w1_codes[:], w1_plane[:], True, True)
         gather(x_codes[:, 0 : S // 2], x_word_table, offs_list, 0, S // 2)
         gather(x_codes[:, S // 2 : S], x_word_table, offs_list, S // 2, S)
         d_codes = keep.tile([P, V], U32, name="d_codes", tag="x_word_table", align_bytes=64)

from contextlib import ExitStack

import concourse.mybir as mybir

K, T, S, V, H, W = 512, 2048, 512, 512, 512, 1024
FLOPS = 4 * 2 * 512 * 512 * 512

F32 = mybir.dt.float32
BF16 = mybir.dt.bfloat16
I32 = mybir.dt.int32
U32 = mybir.dt.uint32
U16 = mybir.dt.uint16
U8 = mybir.dt.uint8
FP8X4 = mybir.dt.float8_e4m3fn_x4
ACT = mybir.ActivationFunctionType

P = 128
PACK = 4
BLOCKS = 4
HALF = H // 2


def tile_picked_zneumf_sig_p_kernel(
    tc, x_words, x_scales, e_words, e_scales, w1, w2, offs, cand, out
):
    nc = tc.nc
    with ExitStack() as ctx:
        keep = ctx.enter_context(tc.tile_pool(name="keep", bufs=1))
        psum = ctx.enter_context(tc.psum_pool(name="psum", bufs=1))

        def sbuf(name, shape, dtype):
            return keep.tile(shape, dtype, name=name, align_bytes=64)

        cand_list = keep.tile([P, V // 16], U16, name="cand_list")
        offs_list = keep.tile([P, S // 16], U16, name="offs_list")
        e_scale_table = sbuf("e_scale_table", [P, W], U8)
        x_scale_table = sbuf("x_scale_table", [P, T], U8)
        e_word_table = sbuf("e_word_table", [P, W], U32)
        x_word_table = sbuf("x_word_table", [P, T], U32)
        warm = sbuf("warm", [P, 2], F32)

        nc.vector.memset(e_scale_table[:].bitcast(I32), 0)
        nc.vector.memset(x_scale_table[:].bitcast(I32), 0)
        nc.vector.memset(warm[:, 0:1], 0.0)
        nc.scalar.activation(warm[:, 1:2], warm[:, 0:1], ACT.Sigmoid)

        def load_scales(table, first, scales):
            for r in range(4):
                nc.sync.dma_start(
                    out=table[first + r : P : 32, :].bitcast(I32),
                    in_=scales[0].rearrange("(q r) c -> r q c", r=4)[r].bitcast(I32),
                )

        def load_words(table, words):
            nc.sync.dma_start(out=table[:].bitcast(I32), in_=words[0].rearrange("p n t -> p (n t)").bitcast(I32))

        def load_weight(name, w, a, b):
            raw = sbuf(name, [P, PACK, b - a], F32)
            nc.sync.dma_start(out=raw[:], in_=w.rearrange("(p j) c -> p j c", j=PACK)[:, :, a:b])
            return raw

        def round_weight(copy, grouped, raw, first, a, b, slots=slice(0, PACK)):
            words = grouped[:, slots, a // PACK : b // PACK, :]
            copy(
                words.rearrange("p s (u r) j -> p s u j r", r=4),
                raw[:, :, a - first : b - first].rearrange("p j (u s r) -> p s u j r", s=PACK, r=4)[:, slots],
            )

        def quantize(codes, scales, values):
            nc.vector.quantize_mx(out=codes.bitcast(FP8X4), scales=scales, in_=values)

        def mx(acc, lhs, lhs_scale, rhs, rhs_scale, start, stop):
            nc.tensor.matmul_mx(
                out=acc, lhsT=lhs.bitcast(FP8X4), lhsT_scale=lhs_scale, rhs=rhs.bitcast(FP8X4), rhs_scale=rhs_scale,
                start=start, stop=stop,
            )

        def gather(dst, table, offsets, a, b):
            nc.vector.tensor_copy(dst, table[:].indirect(offsets[:, a // 16 : b // 16]))

        def relu_scalar(dst, src):
            nc.scalar.activation(dst, src, ACT.Relu)

        def relu_vector(dst, src):
            nc.vector.tensor_scalar_max(dst, src, 0.0)

        def tower_block(name, tag, w_codes, w_scales, codes, scales):
            acc = psum.tile([P, PACK, P], F32, name=name, tag=tag)
            for s in range(PACK):
                slot = slice(s * P, (s + 1) * P)
                mx(acc[:, s, :], w_codes[:, slot], w_scales[:, slot], codes, scales, True, True)
            return acc[:].rearrange("p s t -> p t s")

        e_codes = sbuf("e_codes", [P, V], U32)
        e_tile = sbuf("e_tile", [P, V], U8)
        x_codes = sbuf("x_codes", [P, S], U32)
        w1_grouped = sbuf("w1_grouped", [P, PACK, P, PACK], BF16)
        w2_grouped = sbuf("w2_grouped", [P, PACK, P, PACK], BF16)
        w1_codes = sbuf("w1_codes", [P, H], U32)
        w1_plane = sbuf("w1_plane", [P, H], U8)
        w2_codes = sbuf("w2_codes", [P, H], U32)
        w2_plane = sbuf("w2_plane", [P, H], U8)
        d_plane = sbuf("d_plane", [P, V], U8)
        p_codes = sbuf("p_codes", [P, S], U32)
        p_plane = sbuf("p_plane", [P, S], U8)

        load_words(e_word_table, e_words)
        nc.sync.dma_start(cand_list[:], cand)
        nc.sync.dma_start(offs_list[:], offs)
        load_scales(e_scale_table, 4, e_scales)
        w2_raw = load_weight("w2_raw", w2, 0, H)
        load_scales(x_scale_table, 0, x_scales)
        w1_raw = load_weight("w1_raw", w1, 0, H)
        load_words(x_word_table, x_words)

        gather(e_codes[:], e_word_table, cand_list, 0, V)
        gather(e_tile[:], e_scale_table, cand_list, 0, V)
        e_plane = e_tile[4:P, :]
        round_weight(nc.scalar.copy, w2_grouped, w2_raw, 0, 0, 256)
        round_weight(nc.vector.tensor_copy, w2_grouped, w2_raw, 0, 256, H)
        x_plane_a = sbuf("x_plane_a", [P, S // 2], U8)
        gather(x_plane_a[:], x_scale_table, offs_list, 0, S // 2)
        quantize(w2_codes[:], w2_plane[:], w2_grouped[:].rearrange("p s m j -> p (s m j)"))
        x_plane_b = keep.tile([P, S // 2], U8, name="x_plane_b", tag="w2_grouped", align_bytes=64)
        gather(x_plane_b[:], x_scale_table, offs_list, S // 2, S)
        x_planes = [x_plane_a[:, 0:P], x_plane_a[:, P : 2 * P], x_plane_b[:, 0:P], x_plane_b[:, P : 2 * P]]
        for h in range(2):
            round_weight(nc.vector.tensor_copy, w1_grouped, w1_raw, 0, 0, H, slice(2 * h, 2 * h + 2))
        for h in range(2):
            cols = slice(h * HALF, (h + 1) * HALF)
            quantize(w1_codes[:, cols], w1_plane[:, cols], w1_grouped[:, 2 * h : 2 * h + 2].rearrange("p s m j -> p (s m j)"))
        d_hidden = sbuf("d_hidden", [P, V, PACK], BF16)
        blocks = [slice(b * P, (b + 1) * P) for b in range(BLOCKS)]
        for b, cols in enumerate(blocks):
            acc = tower_block("d_acc%d" % b, "low%d" % b, w2_codes, w2_plane, e_codes[:, cols], e_plane[:, cols])
            relu_scalar(d_hidden[:, cols, :], acc)
        warm_acc = psum.tile([P, H], F32, name="warm_acc", tag="high3")
        for w in range(2):
            mx(warm_acc[:], w1_codes[:, 0:P], w1_plane[:, 0:P], w1_codes[:], w1_plane[:], True, True)
        gather(x_codes[:, 0 : S // 2], x_word_table, offs_list, 0, S // 2)
        gather(x_codes[:, S // 2 : S], x_word_table, offs_list, S // 2, S)
        d_codes = keep.tile([P, V], U32, name="d_codes", tag="x_word_table", align_bytes=64)
        quantize(d_codes[:], d_plane[:], d_hidden[:].rearrange("p t s -> p (t s)"))
        p_hidden = [sbuf("p_hidden%d" % b, [P, P, PACK], BF16) for b in range(BLOCKS)]
        p_acc = [
            tower_block("p_acc%d" % b, "high%d" % b, w1_codes, w1_plane, x_codes[:, cols], x_planes[b])
            for b, cols in enumerate(blocks)
        ]
        for b in range(BLOCKS - 1):
            relu_scalar(p_hidden[b][:], p_acc[b])
        for b, cols in enumerate(blocks):
            y = psum.tile([P, V], F32, name="y%d" % b, tag="high%d" % b if b else "low0")
            mx(y[:], x_codes[:, cols], x_planes[b], e_codes[:], e_plane, True, False)
            quantize(p_codes[:, cols], p_plane[:, cols], p_hidden[b][:].rearrange("p t s -> p (t s)"))
            if b < 2:
                half = slice(b * P // 2, (b + 1) * P // 2)
                relu_vector(p_hidden[BLOCKS - 1][:, half, :], p_acc[BLOCKS - 1][:, half, :])
            mx(y[:], p_codes[:, cols], p_plane[:, cols], d_codes[:], d_plane[:], False, True)
            scores = sbuf("scores%d" % b, [P, V], F32)
            nc.scalar.activation(scores[:], y[:], ACT.Sigmoid)
            nc.sync.dma_start(out=out[cols, :], in_=scores[:])
